import numpy as np
import ml_dtypes


def mxq(x, axis, fmt="e4m3"):
    dtype, down = {"e4m3": (ml_dtypes.float8_e4m3fn, 7), "e5m2": (ml_dtypes.float8_e5m2, 14)}[fmt]
    v = np.moveaxis(np.asarray(x, np.float32).astype(ml_dtypes.bfloat16).astype(np.float64), axis, -1)
    blocks = v.reshape(v.shape[:-1] + (-1, 32))
    amax = np.abs(blocks).max(-1, keepdims=True)
    byte = np.maximum(np.where(amax > 0, np.frexp(amax)[1] - 1 + 127, 0) - down, 1)
    scale = np.exp2(byte - 127.0)
    codes = (blocks / scale).astype(np.float32).astype(dtype).astype(np.float64)
    return np.moveaxis((codes * scale).reshape(v.shape), -1, axis)


WIDE = False


def mx_kscale(k):
    if not WIDE:
        return np.ones(k)
    levels = np.array([10, -10, 5, -5, 0])
    if k % 512:
        return np.exp2(np.random.permutation(np.resize(levels, k // 32))).repeat(32)
    a = np.empty((k // 512, 16))
    for p in range(k // 512):
        a[p, :8] = np.random.permutation(np.resize(levels, 8))
        for g in range(8):
            far = levels[np.abs(levels - a[p, g]) >= 10]
            a[p, g + 8] = far[np.random.randint(len(far))]
    return np.exp2(a.ravel()).repeat(32)


def f64(x):
    return np.asarray(x).astype(np.float64)


def striped(idx):
    return np.tile(idx.reshape(-1, 16).T, (8, 1)).astype(np.uint16)


def unstriped(offs):
    return offs[:16].T.reshape(-1).astype(np.int64)


def striped8(idx):
    return np.concatenate([x.reshape(-1, 16).T for x in idx]).astype(np.uint16)


def runs(offs, k):
    lists = np.stack([offs[16 * r : 16 * r + 16].T.reshape(-1) for r in range(8)]).astype(np.int64)
    return lists[np.arange(k) % 512 // 64]


def pack_weight(w):
    k, n = w.shape
    w = f64(np.asarray(w, np.float32).astype(ml_dtypes.bfloat16)).reshape(k // 32, 32, n)
    amax = np.abs(w).max(1)
    byte = np.clip(np.where(amax > 0, np.frexp(amax)[1] - 1 + 127 - 7, 1), 1, 254)
    scaled = (w * np.exp2(127.0 - byte)[:, None, :]).reshape(k, n).astype(np.float32)
    words = np.ascontiguousarray(scaled.reshape(k // 512, 128, 4, n).transpose(0, 1, 3, 2)).astype(ml_dtypes.float8_e4m3fn).view(np.uint8)
    return words, np.ascontiguousarray(byte.astype(np.uint8).reshape(k // 512, 16, n))


def unpack_weight(words, scales):
    g, p, n, _ = words.shape
    vals = np.ascontiguousarray(words).view(ml_dtypes.float8_e4m3fn).astype(np.float64) * np.repeat(np.exp2(scales.astype(np.float64) - 127.0), 8, axis=1)[..., None]
    return vals.transpose(0, 1, 3, 2).reshape(g * 512, n)


def sigmoid(v):
    return 1.0 / (1.0 + np.exp(-np.maximum(v, -700.0)))


K, T, S, N, G, H = 512, 2048, 512, 512, 2048, 512


def setup_inputs():
    n = np.random.standard_normal
    s = mx_kscale(K)[:, None]
    u = mx_kscale(S)
    packed_xT = pack_weight(n((K, T)) * s)
    packed_dT = pack_weight(n((K, G)) / s)
    return {
        "x_words": packed_xT[0],
        "x_scales": packed_xT[1],
        "d_words": packed_dT[0],
        "d_scales": packed_dT[1],
        "gn": (np.random.uniform(0.5, 1.5, (H, 1)) * u[:, None]).astype(np.float32),
        "w1": (n((H, N)) / np.sqrt(H) / u[:, None]).astype(np.float32),
        "offs": striped8(np.random.randint(0, T, (8, S))),
        "k1": striped8(np.random.randint(0, G, (8, H))),
        "n1": striped(np.random.permutation(S)),
        "n2": striped(np.random.permutation(S)),
        "n3": striped(np.random.permutation(S)),
    }


def reference(x_words, x_scales, d_words, d_scales, gn, w1, offs, k1, n1, n2, n3):
    d_k1 = unpack_weight(d_words, d_scales)[np.arange(K)[:, None], runs(k1, K)]
    xq = unpack_weight(x_words, x_scales)[np.arange(K)[:, None], runs(offs, K)]
    h = 0.0625 * (d_k1.T @ xq)
    st = h * (sigmoid(h[:, unstriped(n1)]))
    z = f64(gn) * (np.maximum(st, st[:, unstriped(n1)]))
    h2 = mxq(f64(w1), 0, "e4m3").T @ mxq(z, 0, "e4m3")
    return np.minimum(np.maximum(h2, h2[:, unstriped(n2)]), h2[:, unstriped(n3)])

@@ -1,0 +1,226 @@
+from contextlib import ExitStack
+
+import concourse.mybir as mybir
+
+FLOPS = 2 * 2 * 512 * 512 * 512
+
+F32 = mybir.dt.float32
+BF16 = mybir.dt.bfloat16
+I32 = mybir.dt.int32
+U32 = mybir.dt.uint32
+U16 = mybir.dt.uint16
+U8 = mybir.dt.uint8
+FP8X4 = mybir.dt.float8_e4m3fn_x4
+ALU = mybir.AluOpType
+ACT = mybir.ActivationFunctionType
+
+P = 128
+PACK = 4
+TABLE = 2048
+S = 512
+HALF = 256
+CHUNKS = (128, 128, 128, 64, 64)
+
+
+def entries(lst, start, count):
+    return lst[:, start // 16 : (start + count) // 16]
+
+
+def tile_picked_hpqtwicpminmx_none_p_kernel(
+    tc, x_words, x_scales, d_words, d_scales, gn, w1, offs, k1, n1, n2, n3, out
+):
+    nc = tc.nc
+    with ExitStack() as ctx:
+        keep = ctx.enter_context(tc.tile_pool(name="keep", bufs=1))
+        psum = ctx.enter_context(tc.psum_pool(name="psum", bufs=1))
+
+        def load_list(src, name):
+            lst = keep.tile([P, S // 16], U16, name=name)
+            nc.sync.dma_start(lst[:], src)
+            return lst
+
+        def load_scale_table(src, name, engine, queue):
+            table = keep.tile([P, TABLE], U8, name=name)
+            engine.memset(table[:].bitcast(I32), 0)
+            queue.dma_start(table[0:P:8, :].bitcast(I32), src[0].bitcast(I32))
+            return table
+
+        def load_word_table(src, name):
+            table = keep.tile([P, TABLE], U32, name=name)
+            nc.sync.dma_start(table[:].bitcast(I32), src[0].rearrange("p n t -> p (n t)").bitcast(I32))
+            return table
+
+        k1_list = load_list(k1, "k1_list")
+        offs_list = load_list(offs, "offs_list")
+        n1_list = load_list(n1, "n1_list")
+        n2_list = load_list(n2, "n2_list")
+        n3_list = load_list(n3, "n3_list")
+        d_scale_table = load_scale_table(d_scales, "d_scale_table", nc.gpsimd, nc.scalar)
+        x_scale_table = load_scale_table(x_scales, "x_scale_table", nc.vector, nc.scalar)
+        d_table = load_word_table(d_words, "d_table")
+        x_table = load_word_table(x_words, "x_table")
+        gain = keep.tile([P, PACK], F32)
+        nc.gpsimd.dma_start(gain[:], gn.rearrange("(p t) o -> p (t o)", t=PACK))
+
+        d_bytes = keep.tile([P, S], U8, align_bytes=64)
+        x_bytes = keep.tile([P, S], U8, align_bytes=64)
+        planes = keep.tile([P, 2 * S], U8, align_bytes=64)
+        nc.vector.tensor_copy(d_bytes[:], d_scale_table[:].indirect(k1_list[:]))
+        nc.vector.tensor_copy(
+            planes[:, S:].rearrange("p (t c i) -> p c t i", t=PACK, i=16),
+            d_bytes[:].rearrange("p (c i t) -> p c t i", t=PACK, i=16),
+        )
+        nc.vector.tensor_copy(x_bytes[:], x_scale_table[:].indirect(offs_list[:]))
+        nc.vector.tensor_copy(planes[:, :S].bitcast(I32), x_bytes[:].bitcast(I32))
+        for a in range(1, 4):
+            nc.scalar.dma_start(planes[a:P:32, :].bitcast(I32), planes[8 * a : P : 32, :].bitcast(I32))
+
+        w_raw = keep.tile([P, PACK, S], F32, tag="d_scale_table")
+        nc.sync.dma_start(w_raw[:], w1.rearrange("(p t) m -> p t m", t=PACK))
+
+        d_picked = keep.tile([P, S], U32, tag="x_bytes", align_bytes=64)
+        d_codes = keep.tile([P, S], U32, align_bytes=64)
+        x_codes = keep.tile([P, S], U32, tag="d_bytes", align_bytes=64)
+        nc.vector.tensor_copy(d_picked[:], d_table[:].indirect(k1_list[:]))
+        nc.vector.tensor_copy(
+            d_codes[:].rearrange("p (t c i) -> p c t i", t=PACK, i=4),
+            d_picked[:].rearrange("p (c i t) -> p c t i", t=PACK, i=4),
+        )
+        for j0 in (0, HALF):
+            nc.vector.tensor_copy(x_codes[:, j0 : j0 + HALF], x_table[:].indirect(entries(offs_list, j0, HALF)))
+
+        sign = keep.tile([P, PACK], F32)
+        above = keep.tile([P, PACK], F32)
+        size = keep.tile([P, PACK], F32)
+        factor = keep.tile([P, PACK], F32)
+        nc.gpsimd.tensor_scalar(above[:], gain[:], 0.0, None, ALU.is_ge)
+        nc.gpsimd.tensor_scalar(sign[:], above[:], 2.0, -1.0, ALU.mult, ALU.add)
+        nc.gpsimd.tensor_tensor(size[:], gain[:], sign[:], ALU.mult)
+        nc.gpsimd.tensor_scalar(factor[:], size[:], 0.0625, 0.0, ALU.mult, ALU.add)
+
+        def first_product(acc, t, j0, n):
+            nc.tensor.matmul_mx(
+                out=acc,
+                lhsT=d_codes[:, P * t : P * (t + 1)].bitcast(FP8X4),
+                lhsT_scale=planes[:, S + P * t : S + P * (t + 1)],
+                rhs=x_codes[:, j0 : j0 + n].bitcast(FP8X4),
+                rhs_scale=planes[:, j0 : j0 + n],
+                start=True,
+                stop=True,
+            )
+
+        sums = {}
+        window = [keep.tile([P, S], F32, name="window%d" % t) for t in range(PACK)]
+        for hf, j0 in enumerate((0, HALF)):
+            acc = psum.tile([P, HALF], F32, name="bank%d" % hf)
+            first_product(acc[:], 0, j0, HALF)
+            sums[0, j0] = acc[:]
+            nc.scalar.activation(window[0][:, j0 : j0 + HALF], acc[:], ACT.Sigmoid, scale=0.0625)
+        for t in range(1, PACK):
+            acc = psum.tile([P, S], F32, name="bank%d" % (t + 1))
+            first_product(acc[:], t, 0, S)
+            for j0 in (0, HALF):
+                sums[t, j0] = acc[:, j0 : j0 + HALF]
+            nc.vector.tensor_scalar(window[t][:], acc[:], 0.0625, None, ALU.mult)
+
+        st = keep.tile([P, PACK, S], F32, tag="d_codes", align_bytes=64)
+        w_codes = keep.tile([P, S], U32, align_bytes=64)
+        w_scales = keep.tile([P, S], U8, align_bytes=64)
+        w_grouped = keep.tile([P, S * PACK], BF16, tag="d_bytes", align_bytes=64)
+
+        def group_w(m):
+            nc.vector.tensor_tensor(
+                w_grouped[:, PACK * P * m : PACK * P * (m + 1)].rearrange("p (c i t) -> p c t i", t=PACK, i=4),
+                w_raw[:, :, P * m : P * (m + 1)].rearrange("p t (c i) -> p c t i", i=4),
+                sign[:].unsqueeze(1).unsqueeze(3).to_broadcast([P, P // 4, PACK, 4]),
+                ALU.mult,
+            )
+
+        for t in range(PACK):
+            for j0 in (0, HALF):
+                gate = keep.tile([P, HALF], F32, name="gate%d_%d" % (t, j0))
+                nc.scalar.activation(
+                    gate[:],
+                    window[t][:].indirect(entries(n1_list, j0, HALF)),
+                    ACT.Copy if t == 0 else ACT.Sigmoid,
+                )
+                nc.vector.scalar_tensor_tensor(
+                    st[:, t, j0 : j0 + HALF],
+                    sums[t, j0],
+                    factor[:, t : t + 1],
+                    gate[:],
+                    ALU.mult,
+                    ALU.mult,
+                )
+                if t in (1, 2) and j0 == 0:
+                    group_w(t - 1)
+        group_w(2)
+        group_w(3)
+
+        nc.vector.quantize_mx(out=w_codes[:].bitcast(FP8X4), scales=w_scales[:], in_=w_grouped[:])
+
+        h2 = keep.tile([P, PACK, S], F32)
+        st_far_all = keep.tile([P, PACK * S], F32, name="st_far", tag="gate3_0")
+        j0 = 0
+        pending = []
+        for c, n in enumerate(CHUNKS):
+            st_far = st_far_all[:, PACK * j0 : PACK * (j0 + n)].rearrange("p (t j) -> p t j", t=PACK)
+            for t in range(PACK):
+                nc.scalar.activation(st_far[:, t, :], st[:, t, :].indirect(entries(n1_list, j0, n)), ACT.Copy)
+            z = keep.tile([P, n * PACK], BF16, name="z", align_bytes=64)
+            nc.vector.tensor_tensor(
+                z[:].rearrange("p (c i t) -> p c t i", t=PACK, i=4),
+                st[:, :, j0 : j0 + n].rearrange("p t (c i) -> p c t i", i=4),
+                st_far.rearrange("p t (c i) -> p c t i", i=4),
+                ALU.max,
+            )
+            z_codes = keep.tile([P, n], U32, name="z_codes%d" % c, align_bytes=64)
+            z_scales = keep.tile([P, n], U8, name="z_scales%d" % c, align_bytes=64)
+            nc.vector.quantize_mx(out=z_codes[:].bitcast(FP8X4), scales=z_scales[:], in_=z[:])
+            last = c == len(CHUNKS) - 1
+            for b, ms in enumerate(((0,), (1, 2, 3)) if last else ((0, 1, 2, 3),)):
+                acc = psum.tile([P, len(ms), n], F32, name="bank%d" % ((5 + c + b) % 8))
+                for i, m in enumerate(ms):
+                    nc.tensor.matmul_mx(
+                        out=acc[:, i, :],
+                        lhsT=w_codes[:, P * m : P * (m + 1)].bitcast(FP8X4),
+                        lhsT_scale=w_scales[:, P * m : P * (m + 1)],
+                        rhs=z_codes[:].bitcast(FP8X4),
+                        rhs_scale=z_scales[:],
+                        start=True,
+                        stop=True,
+                    )
+                dst = h2[:, ms[0] : ms[-1] + 1, j0 : j0 + n]
+                if c == 0 or (last and b == 1):
+                    nc.vector.tensor_copy(dst, acc[:])
+                else:
+                    pending.append((dst, acc))
+            j0 = j0 + n
+        for dst, acc in pending:
+            nc.scalar.copy(dst, acc[:])
+
+        by_n2 = keep.tile([P, PACK, S], F32)
+        by_n3 = keep.tile([P, PACK, S], F32)
+        larger = keep.tile([P, PACK, S], F32)
+        result = keep.tile([P, PACK, S], F32)
+
+        def fetch(engine, dst, lst, m):
+            for j0 in (0, HALF):
+                picked = h2[:, m, :].indirect(entries(lst, j0, HALF))
+                if engine == "vector":
+                    nc.vector.tensor_copy(dst[:, m, j0 : j0 + HALF], picked)
+                else:
+                    nc.scalar.activation(dst[:, m, j0 : j0 + HALF], picked, ACT.Copy)
+
+        for m in range(PACK):
+            if m % 2 == 1:
+                fetch("scalar", by_n2, n2_list, m)
+            if m == 0:
+                fetch("vector", by_n2, n2_list, 0)
+            if m == 1:
+                fetch("vector", by_n2, n2_list, 2)
+            fetch("scalar", by_n3, n3_list, m)
+            nc.vector.tensor_tensor(larger[:, m, :], h2[:, m, :], by_n2[:, m, :], ALU.max)
+            for cols in (slice(0, S),) if m < PACK - 1 else (slice(0, HALF), slice(HALF, S)):
+                nc.vector.tensor_tensor(result[:, m, cols], larger[:, m, cols], by_n3[:, m, cols], ALU.min)
+                nc.sync.dma_start(out[P * m : P * (m + 1), cols], result[:, m, cols])

@@ -19,7 +19,7 @@ PACK = 4
 TABLE = 2048
 S = 512
 HALF = 256
-CHUNKS = (128, 128, 128, 64, 64)
+CHUNKS = (256, 128, 128)
 
 
 def entries(lst, start, count):
@@ -39,10 +39,10 @@ def tile_picked_hpqtwicpminmx_none_p_kernel(
             nc.sync.dma_start(lst[:], src)
             return lst
 
-        def load_scale_table(src, name, engine, queue):
+        def load_scale_table(src, name, engine):
             table = keep.tile([P, TABLE], U8, name=name)
             engine.memset(table[:].bitcast(I32), 0)
-            queue.dma_start(table[0:P:8, :].bitcast(I32), src[0].bitcast(I32))
+            nc.sync.dma_start(table[0:P:8, :].bitcast(I32), src[0].bitcast(I32))
             return table
 
         def load_word_table(src, name):
@@ -55,8 +55,8 @@ def tile_picked_hpqtwicpminmx_none_p_kernel(
         n1_list = load_list(n1, "n1_list")
         n2_list = load_list(n2, "n2_list")
         n3_list = load_list(n3, "n3_list")
-        d_scale_table = load_scale_table(d_scales, "d_scale_table", nc.gpsimd, nc.scalar)
-        x_scale_table = load_scale_table(x_scales, "x_scale_table", nc.vector, nc.scalar)
+        d_scale_table = load_scale_table(d_scales, "d_scale_table", nc.vector)
+        x_scale_table = load_scale_table(x_scales, "x_scale_table", nc.gpsimd)
         d_table = load_word_table(d_words, "d_table")
         x_table = load_word_table(x_words, "x_table")
         gain = keep.tile([P, PACK], F32)
@@ -75,9 +75,6 @@ def tile_picked_hpqtwicpminmx_none_p_kernel(
         for a in range(1, 4):
             nc.scalar.dma_start(planes[a:P:32, :].bitcast(I32), planes[8 * a : P : 32, :].bitcast(I32))
 
-        w_raw = keep.tile([P, PACK, S], F32, tag="d_scale_table")
-        nc.sync.dma_start(w_raw[:], w1.rearrange("(p t) m -> p t m", t=PACK))
-
         d_picked = keep.tile([P, S], U32, tag="x_bytes", align_bytes=64)
         d_codes = keep.tile([P, S], U32, align_bytes=64)
         x_codes = keep.tile([P, S], U32, tag="d_bytes", align_bytes=64)
@@ -86,6 +83,8 @@ def tile_picked_hpqtwicpminmx_none_p_kernel(
             d_codes[:].rearrange("p (t c i) -> p c t i", t=PACK, i=4),
             d_picked[:].rearrange("p (c i t) -> p c t i", t=PACK, i=4),
         )
+        w_raw = keep.tile([P, PACK, S], F32, tag="d_table")
+        nc.sync.dma_start(w_raw[:], w1.rearrange("(p t) m -> p t m", t=PACK))
         for j0 in (0, HALF):
             nc.vector.tensor_copy(x_codes[:, j0 : j0 + HALF], x_table[:].indirect(entries(offs_list, j0, HALF)))
 
@@ -110,7 +109,10 @@ def tile_picked_hpqtwicpminmx_none_p_kernel(
             )
 
         sums = {}
-        window = [keep.tile([P, S], F32, name="window%d" % t) for t in range(PACK)]
+        widths = (S + 16, 2 * S, 2 * S, S)
+        window = [keep.tile([P, widths[t]], F32, name="window%d" % t) for t in range(PACK)]
+        for t in range(PACK - 1):
+            nc.gpsimd.memset(window[t][:, S:], 0.0)
         for hf, j0 in enumerate((0, HALF)):
             acc = psum.tile([P, HALF], F32, name="bank%d" % hf)
             first_product(acc[:], 0, j0, HALF)
@@ -119,9 +121,8 @@ def tile_picked_hpqtwicpminmx_none_p_kernel(
         for t in range(1, PACK):
             acc = psum.tile([P, S], F32, name="bank%d" % (t + 1))
             first_product(acc[:], t, 0, S)
-            for j0 in (0, HALF):
-                sums[t, j0] = acc[:, j0 : j0 + HALF]
-            nc.vector.tensor_scalar(window[t][:], acc[:], 0.0625, None, ALU.mult)
+            sums[t] = acc
+            nc.vector.tensor_scalar(window[t][:, :S], acc[:], 0.0625, None, ALU.mult)
 
         st = keep.tile([P, PACK, S], F32, tag="d_codes", align_bytes=64)
         w_codes = keep.tile([P, S], U32, align_bytes=64)
@@ -136,24 +137,26 @@ def tile_picked_hpqtwicpminmx_none_p_kernel(
                 ALU.mult,
             )
 
+        def gated(t, j0, n, acc, gate):
+            nc.vector.scalar_tensor_tensor(
+                st[:, t, j0 : j0 + n], acc, factor[:, t : t + 1], gate, ALU.mult, ALU.mult
+            )
+
         for t in range(PACK):
-            for j0 in (0, HALF):
-                gate = keep.tile([P, HALF], F32, name="gate%d_%d" % (t, j0))
+            for j0, n in ((0, S),) if t < PACK - 1 else ((0, HALF), (HALF, HALF)):
+                gate = keep.tile([P, n], F32, name="gate%d_%d" % (t, j0))
                 nc.scalar.activation(
                     gate[:],
-                    window[t][:].indirect(entries(n1_list, j0, HALF)),
+                    window[t][:].indirect(entries(n1_list, j0, n)),
                     ACT.Copy if t == 0 else ACT.Sigmoid,
                 )
-                nc.vector.scalar_tensor_tensor(
-                    st[:, t, j0 : j0 + HALF],
-                    sums[t, j0],
-                    factor[:, t : t + 1],
-                    gate[:],
-                    ALU.mult,
-                    ALU.mult,
-                )
-                if t in (1, 2) and j0 == 0:
-                    group_w(t - 1)
+                if t == 0:
+                    for i0 in (0, HALF):
+                        gated(0, i0, HALF, sums[0, i0], gate[:, i0 : i0 + HALF])
+                else:
+                    gated(t, j0, n, sums[t][:, j0 : j0 + n], gate[:])
+            if t < 2:
+                group_w(t)
         group_w(2)
         group_w(3)
 
@@ -178,8 +181,9 @@ def tile_picked_hpqtwicpminmx_none_p_kernel(
             z_scales = keep.tile([P, n], U8, name="z_scales%d" % c, align_bytes=64)
             nc.vector.quantize_mx(out=z_codes[:].bitcast(FP8X4), scales=z_scales[:], in_=z[:])
             last = c == len(CHUNKS) - 1
-            for b, ms in enumerate(((0,), (1, 2, 3)) if last else ((0, 1, 2, 3),)):
-                acc = psum.tile([P, len(ms), n], F32, name="bank%d" % ((5 + c + b) % 8))
+            groups = (((0, 1), (2, 3)), ((0, 1, 2, 3),), ((0,), (1, 2, 3)))[c]
+            for b, ms in enumerate(groups):
+                acc = psum.tile([P, len(ms), n], F32, name="bank%d" % ((5, 7, 0)[c] + b))
                 for i, m in enumerate(ms):
                     nc.tensor.matmul_mx(
                         out=acc[:, i, :],
@@ -191,7 +195,7 @@ def tile_picked_hpqtwicpminmx_none_p_kernel(
                         stop=True,
                     )
                 dst = h2[:, ms[0] : ms[-1] + 1, j0 : j0 + n]
-                if c == 0 or (last and b == 1):
+                if last and b == 1:
                     nc.vector.tensor_copy(dst, acc[:])
                 else:
                     pending.append((dst, acc))
@@ -204,13 +208,17 @@ def tile_picked_hpqtwicpminmx_none_p_kernel(
         larger = keep.tile([P, PACK, S], F32)
         result = keep.tile([P, PACK, S], F32)
 
+        h2_flat = h2[:].rearrange("p m j -> p (m j)")
+
         def fetch(engine, dst, lst, m):
-            for j0 in (0, HALF):
-                picked = h2[:, m, :].indirect(entries(lst, j0, HALF))
+            whole = m in (1, 2)
+            span = (704 if engine == "vector" else 2 * S) if whole else S
+            for j0, n in ((0, S),) if whole else ((0, HALF), (HALF, HALF)):
+                picked = h2_flat[:, S * m : S * m + span].indirect(entries(lst, j0, n))
                 if engine == "vector":
-                    nc.vector.tensor_copy(dst[:, m, j0 : j0 + HALF], picked)
+                    nc.vector.tensor_copy(dst[:, m, j0 : j0 + n], picked)
                 else:
-                    nc.scalar.activation(dst[:, m, j0 : j0 + HALF], picked, ACT.Copy)
+                    nc.scalar.activation(dst[:, m, j0 : j0 + n], picked, ACT.Copy)
 
         for m in range(PACK):
             if m % 2 == 1:

from contextlib import ExitStack

import concourse.mybir as mybir

FLOPS = 2 * 2 * 512 * 512 * 512

F32 = mybir.dt.float32
BF16 = mybir.dt.bfloat16
I32 = mybir.dt.int32
U32 = mybir.dt.uint32
U16 = mybir.dt.uint16
U8 = mybir.dt.uint8
FP8X4 = mybir.dt.float8_e4m3fn_x4
ALU = mybir.AluOpType
ACT = mybir.ActivationFunctionType

P = 128
PACK = 4
TABLE = 2048
S = 512
HALF = 256
CHUNKS = (256, 128, 128)


def entries(lst, start, count):
    return lst[:, start // 16 : (start + count) // 16]


def tile_picked_hpqtwicpminmx_none_p_kernel(
    tc, x_words, x_scales, d_words, d_scales, gn, w1, offs, k1, n1, n2, n3, out
):
    nc = tc.nc
    with ExitStack() as ctx:
        keep = ctx.enter_context(tc.tile_pool(name="keep", bufs=1))
        psum = ctx.enter_context(tc.psum_pool(name="psum", bufs=1))

        def load_list(src, name):
            lst = keep.tile([P, S // 16], U16, name=name)
            nc.sync.dma_start(lst[:], src)
            return lst

        def load_scale_table(src, name, engine):
            table = keep.tile([P, TABLE], U8, name=name)
            engine.memset(table[:].bitcast(I32), 0)
            nc.sync.dma_start(table[0:P:8, :].bitcast(I32), src[0].bitcast(I32))
            return table

        def load_word_table(src, name):
            table = keep.tile([P, TABLE], U32, name=name)
            nc.sync.dma_start(table[:].bitcast(I32), src[0].rearrange("p n t -> p (n t)").bitcast(I32))
            return table

        k1_list = load_list(k1, "k1_list")
        offs_list = load_list(offs, "offs_list")
        n1_list = load_list(n1, "n1_list")
        n2_list = load_list(n2, "n2_list")
        n3_list = load_list(n3, "n3_list")
        d_scale_table = load_scale_table(d_scales, "d_scale_table", nc.vector)
        x_scale_table = load_scale_table(x_scales, "x_scale_table", nc.gpsimd)
        d_table = load_word_table(d_words, "d_table")
        x_table = load_word_table(x_words, "x_table")
        gain = keep.tile([P, PACK], F32)
        nc.gpsimd.dma_start(gain[:], gn.rearrange("(p t) o -> p (t o)", t=PACK))

        d_bytes = keep.tile([P, S], U8, align_bytes=64)
        x_bytes = keep.tile([P, S], U8, align_bytes=64)
        planes = keep.tile([P, 2 * S], U8, align_bytes=64)
        nc.vector.tensor_copy(d_bytes[:], d_scale_table[:].indirect(k1_list[:]))
        nc.vector.tensor_copy(
            planes[:, S:].rearrange("p (t c i) -> p c t i", t=PACK, i=16),
            d_bytes[:].rearrange("p (c i t) -> p c t i", t=PACK, i=16),
        )
        nc.vector.tensor_copy(x_bytes[:], x_scale_table[:].indirect(offs_list[:]))
        nc.vector.tensor_copy(planes[:, :S].bitcast(I32), x_bytes[:].bitcast(I32))
        for a in range(1, 4):
            nc.scalar.dma_start(planes[a:P:32, :].bitcast(I32), planes[8 * a : P : 32, :].bitcast(I32))

        d_picked = keep.tile([P, S], U32, tag="x_bytes", align_bytes=64)
        d_codes = keep.tile([P, S], U32, align_bytes=64)
        x_codes = keep.tile([P, S], U32, tag="d_bytes", align_bytes=64)
        nc.vector.tensor_copy(d_picked[:], d_table[:].indirect(k1_list[:]))
        nc.vector.tensor_copy(
            d_codes[:].rearrange("p (t c i) -> p c t i", t=PACK, i=4),
            d_picked[:].rearrange("p (c i t) -> p c t i", t=PACK, i=4),
        )
        w_raw = keep.tile([P, PACK, S], F32, tag="d_table")
        nc.sync.dma_start(w_raw[:], w1.rearrange("(p t) m -> p t m", t=PACK))
        for j0 in (0, HALF):
            nc.vector.tensor_copy(x_codes[:, j0 : j0 + HALF], x_table[:].indirect(entries(offs_list, j0, HALF)))

        sign = keep.tile([P, PACK], F32)
        above = keep.tile([P, PACK], F32)
        size = keep.tile([P, PACK], F32)
        factor = keep.tile([P, PACK], F32)
        nc.gpsimd.tensor_scalar(above[:], gain[:], 0.0, None, ALU.is_ge)
        nc.gpsimd.tensor_scalar(sign[:], above[:], 2.0, -1.0, ALU.mult, ALU.add)
        nc.gpsimd.tensor_tensor(size[:], gain[:], sign[:], ALU.mult)
        nc.gpsimd.tensor_scalar(factor[:], size[:], 0.0625, 0.0, ALU.mult, ALU.add)

        def first_product(acc, t, j0, n):
            nc.tensor.matmul_mx(
                out=acc,
                lhsT=d_codes[:, P * t : P * (t + 1)].bitcast(FP8X4),
                lhsT_scale=planes[:, S + P * t : S + P * (t + 1)],
                rhs=x_codes[:, j0 : j0 + n].bitcast(FP8X4),
                rhs_scale=planes[:, j0 : j0 + n],
                start=True,
                stop=True,
            )

        sums = {}
        widths = (S + 16, 2 * S, 2 * S, S)
        window = [keep.tile([P, widths[t]], F32, name="window%d" % t) for t in range(PACK)]
        for t in range(PACK - 1):
            nc.gpsimd.memset(window[t][:, S:], 0.0)
        for hf, j0 in enumerate((0, HALF)):
            acc = psum.tile([P, HALF], F32, name="bank%d" % hf)
            first_product(acc[:], 0, j0, HALF)
            sums[0, j0] = acc[:]
            nc.scalar.activation(window[0][:, j0 : j0 + HALF], acc[:], ACT.Sigmoid, scale=0.0625)
        for t in range(1, PACK):
            acc = psum.tile([P, S], F32, name="bank%d" % (t + 1))
            first_product(acc[:], t, 0, S)
            sums[t] = acc
            nc.vector.tensor_scalar(window[t][:, :S], acc[:], 0.0625, None, ALU.mult)

        st = keep.tile([P, PACK, S], F32, tag="d_codes", align_bytes=64)
        w_codes = keep.tile([P, S], U32, align_bytes=64)
        w_scales = keep.tile([P, S], U8, align_bytes=64)
        w_grouped = keep.tile([P, S * PACK], BF16, tag="d_bytes", align_bytes=64)

        def group_w(m):
            nc.vector.tensor_tensor(
                w_grouped[:, PACK * P * m : PACK * P * (m + 1)].rearrange("p (c i t) -> p c t i", t=PACK, i=4),
                w_raw[:, :, P * m : P * (m + 1)].rearrange("p t (c i) -> p c t i", i=4),
                sign[:].unsqueeze(1).unsqueeze(3).to_broadcast([P, P // 4, PACK, 4]),
                ALU.mult,
            )

        def gated(t, j0, n, acc, gate):
            nc.vector.scalar_tensor_tensor(
                st[:, t, j0 : j0 + n], acc, factor[:, t : t + 1], gate, ALU.mult, ALU.mult
            )

        for t in range(PACK):
            for j0, n in ((0, S),) if t < PACK - 1 else ((0, HALF), (HALF, HALF)):
                gate = keep.tile([P, n], F32, name="gate%d_%d" % (t, j0))
                nc.scalar.activation(
                    gate[:],
                    window[t][:].indirect(entries(n1_list, j0, n)),
                    ACT.Copy if t == 0 else ACT.Sigmoid,
                )
                if t == 0:
                    for i0 in (0, HALF):
                        gated(0, i0, HALF, sums[0, i0], gate[:, i0 : i0 + HALF])
                else:
                    gated(t, j0, n, sums[t][:, j0 : j0 + n], gate[:])
            if t < 2:
                group_w(t)
        group_w(2)
        group_w(3)

        nc.vector.quantize_mx(out=w_codes[:].bitcast(FP8X4), scales=w_scales[:], in_=w_grouped[:])

        h2 = keep.tile([P, PACK, S], F32)
        st_far_all = keep.tile([P, PACK * S], F32, name="st_far", tag="gate3_0")
        j0 = 0
        pending = []
        for c, n in enumerate(CHUNKS):
            st_far = st_far_all[:, PACK * j0 : PACK * (j0 + n)].rearrange("p (t j) -> p t j", t=PACK)
            for t in range(PACK):
                nc.scalar.activation(st_far[:, t, :], st[:, t, :].indirect(entries(n1_list, j0, n)), ACT.Copy)
            z = keep.tile([P, n * PACK], BF16, name="z", align_bytes=64)
            nc.vector.tensor_tensor(
                z[:].rearrange("p (c i t) -> p c t i", t=PACK, i=4),
                st[:, :, j0 : j0 + n].rearrange("p t (c i) -> p c t i", i=4),
                st_far.rearrange("p t (c i) -> p c t i", i=4),
                ALU.max,
            )
            z_codes = keep.tile([P, n], U32, name="z_codes%d" % c, align_bytes=64)
            z_scales = keep.tile([P, n], U8, name="z_scales%d" % c, align_bytes=64)
            nc.vector.quantize_mx(out=z_codes[:].bitcast(FP8X4), scales=z_scales[:], in_=z[:])
            last = c == len(CHUNKS) - 1
            groups = (((0, 1), (2, 3)), ((0, 1, 2, 3),), ((0,), (1, 2, 3)))[c]
            for b, ms in enumerate(groups):
                acc = psum.tile([P, len(ms), n], F32, name="bank%d" % ((5, 7, 0)[c] + b))
                for i, m in enumerate(ms):
                    nc.tensor.matmul_mx(
                        out=acc[:, i, :],
                        lhsT=w_codes[:, P * m : P * (m + 1)].bitcast(FP8X4),
                        lhsT_scale=w_scales[:, P * m : P * (m + 1)],
                        rhs=z_codes[:].bitcast(FP8X4),
                        rhs_scale=z_scales[:],
                        start=True,
                        stop=True,
                    )
                dst = h2[:, ms[0] : ms[-1] + 1, j0 : j0 + n]
                if last and b == 1:
                    nc.vector.tensor_copy(dst, acc[:])
                else:
                    pending.append((dst, acc))
            j0 = j0 + n
        for dst, acc in pending:
            nc.scalar.copy(dst, acc[:])

        by_n2 = keep.tile([P, PACK, S], F32)
        by_n3 = keep.tile([P, PACK, S], F32)
        larger = keep.tile([P, PACK, S], F32)
        result = keep.tile([P, PACK, S], F32)

        h2_flat = h2[:].rearrange("p m j -> p (m j)")

        def fetch(engine, dst, lst, m):
            whole = m in (1, 2)
            span = (704 if engine == "vector" else 2 * S) if whole else S
            for j0, n in ((0, S),) if whole else ((0, HALF), (HALF, HALF)):
                picked = h2_flat[:, S * m : S * m + span].indirect(entries(lst, j0, n))
                if engine == "vector":
                    nc.vector.tensor_copy(dst[:, m, j0 : j0 + n], picked)
                else:
                    nc.scalar.activation(dst[:, m, j0 : j0 + n], picked, ACT.Copy)

        for m in range(PACK):
            if m % 2 == 1:
                fetch("scalar", by_n2, n2_list, m)
            if m == 0:
                fetch("vector", by_n2, n2_list, 0)
            if m == 1:
                fetch("vector", by_n2, n2_list, 2)
            fetch("scalar", by_n3, n3_list, m)
            nc.vector.tensor_tensor(larger[:, m, :], h2[:, m, :], by_n2[:, m, :], ALU.max)
            for cols in (slice(0, S),) if m < PACK - 1 else (slice(0, HALF), slice(HALF, S)):
                nc.vector.tensor_tensor(result[:, m, cols], larger[:, m, cols], by_n3[:, m, cols], ALU.min)
                nc.sync.dma_start(out[P * m : P * (m + 1), cols], result[:, m, cols])
